import numpy as np
import ml_dtypes


def mxq(x, axis, fmt="e4m3"):
    dtype, down = {"e4m3": (ml_dtypes.float8_e4m3fn, 7), "e5m2": (ml_dtypes.float8_e5m2, 14)}[fmt]
    v = np.moveaxis(np.asarray(x, np.float32).astype(ml_dtypes.bfloat16).astype(np.float64), axis, -1)
    blocks = v.reshape(v.shape[:-1] + (-1, 32))
    amax = np.abs(blocks).max(-1, keepdims=True)
    byte = np.maximum(np.where(amax > 0, np.frexp(amax)[1] - 1 + 127, 0) - down, 1)
    scale = np.exp2(byte - 127.0)
    codes = (blocks / scale).astype(np.float32).astype(dtype).astype(np.float64)
    return np.moveaxis((codes * scale).reshape(v.shape), -1, axis)


WIDE = False


def mx_kscale(k):
    if not WIDE:
        return np.ones(k)
    levels = np.array([10, -10, 5, -5, 0])
    if k % 512:
        return np.exp2(np.random.permutation(np.resize(levels, k // 32))).repeat(32)
    a = np.empty((k // 512, 16))
    for p in range(k // 512):
        a[p, :8] = np.random.permutation(np.resize(levels, 8))
        for g in range(8):
            far = levels[np.abs(levels - a[p, g]) >= 10]
            a[p, g + 8] = far[np.random.randint(len(far))]
    return np.exp2(a.ravel()).repeat(32)


def f64(x):
    return np.asarray(x).astype(np.float64)


def striped(idx):
    return np.tile(idx.reshape(-1, 16).T, (8, 1)).astype(np.uint16)


def unstriped(offs):
    return offs[:16].T.reshape(-1).astype(np.int64)


def striped8(idx):
    return np.concatenate([x.reshape(-1, 16).T for x in idx]).astype(np.uint16)


def runs(offs, k):
    lists = np.stack([offs[16 * r : 16 * r + 16].T.reshape(-1) for r in range(8)]).astype(np.int64)
    return lists[np.arange(k) % 512 // 64]


def pack_weight(w):
    k, n = w.shape
    w = f64(np.asarray(w, np.float32).astype(ml_dtypes.bfloat16)).reshape(k // 32, 32, n)
    amax = np.abs(w).max(1)
    byte = np.clip(np.where(amax > 0, np.frexp(amax)[1] - 1 + 127 - 7, 1), 1, 254)
    scaled = (w * np.exp2(127.0 - byte)[:, None, :]).reshape(k, n).astype(np.float32)
    words = np.ascontiguousarray(scaled.reshape(k // 512, 128, 4, n).transpose(0, 1, 3, 2)).astype(ml_dtypes.float8_e4m3fn).view(np.uint8)
    return words, np.ascontiguousarray(byte.astype(np.uint8).reshape(k // 512, 16, n))


def unpack_weight(words, scales):
    g, p, n, _ = words.shape
    vals = np.ascontiguousarray(words).view(ml_dtypes.float8_e4m3fn).astype(np.float64) * np.repeat(np.exp2(scales.astype(np.float64) - 127.0), 8, axis=1)[..., None]
    return vals.transpose(0, 1, 3, 2).reshape(g * 512, n)


def sigmoid(v):
    return 1.0 / (1.0 + np.exp(-np.maximum(v, -700.0)))


K, T, S, H, G, W = 512, 1024, 256, 512, 2048, 128


def setup_inputs():
    n = np.random.standard_normal
    s = mx_kscale(K)[:, None]
    packed_xT = pack_weight(n((K, T)) * s)
    packed_w1 = pack_weight(n((K, H)) / np.sqrt(2 * K) / s)
    packed_w2 = pack_weight(n((K, H)) / np.sqrt(2 * K) / s)
    packed_dT = pack_weight(n((K, G)) / s)
    perm = np.random.permutation(S)
    return {
        "x_words": packed_xT[0],
        "x_scales": packed_xT[1],
        "w1_words": packed_w1[0],
        "w1_scales": packed_w1[1],
        "w2_words": packed_w2[0],
        "w2_scales": packed_w2[1],
        "sl": np.random.uniform(1.0, 2.0, (H, 1)).astype(np.float32),
        "th": (0.5 * n((H, 1))).astype(np.float32),
        "gs": (np.random.uniform(0.5, 1.5, (K, 1)) * s).astype(np.float32),
        "d_words": packed_dT[0],
        "d_scales": packed_dT[1],
        "offs": striped(np.random.permutation(T)[:S]),
        "hz": striped8(np.random.randint(0, T, (8, S))),
        "n1": striped(np.random.permutation(S)),
        "n2": striped(np.random.permutation(S)),
        "n3": striped(np.random.permutation(S)),
        "k1": striped8(np.random.randint(0, G, (8, H))),
        "k2": striped8(np.random.randint(0, G, (8, H))),
        "two": striped(np.random.permutation(T)[:S]),
        "k3": striped8(np.random.randint(0, G, (8, H))),
        "hy": striped8(np.random.randint(0, T, (8, S))),
        "n4": striped(perm[:W]),
        "n5": striped(perm[W:]),
        "n6": striped(np.random.permutation(S)),
    }


def reference(x_words, x_scales, w1_words, w1_scales, w2_words, w2_scales, sl, th, gs, d_words, d_scales, offs, hz, n1, n2, n3, k1, k2, two, k3, hy, n4, n5, n6):
    d_k1 = unpack_weight(d_words, d_scales)[np.arange(K)[:, None], runs(k1, K)]
    xq = unpack_weight(x_words, x_scales)[:, unstriped(offs)]
    x_hz = unpack_weight(x_words, x_scales)[np.arange(K)[:, None], runs(hz, K)]
    y = unpack_weight(w1_words, w1_scales).T @ xq + unpack_weight(w2_words, w2_scales).T @ x_hz
    ds2 = np.zeros((H, S))
    ds2[:, unstriped(n2)] = y
    ds = np.zeros((H, S))
    ds[:, unstriped(n1)] = y
    sg = sigmoid(f64(sl) * (ds[:, unstriped(n3)] - f64(th)))
    z = f64(gs) * (ds2 * sg)
    d_k2 = unpack_weight(d_words, d_scales)[np.arange(K)[:, None], runs(k2, K)]
    x_two = unpack_weight(x_words, x_scales)[:, unstriped(two)]
    d_k3 = unpack_weight(d_words, d_scales)[np.arange(K)[:, None], runs(k3, K)]
    x_hy = unpack_weight(x_words, x_scales)[np.arange(K)[:, None], runs(hy, K)]
    h2 = 0.0625 * ((d_k1.T @ mxq(z, 0, "e4m3") + d_k2.T @ x_two + d_k3.T @ x_hy))
    pa = h2[:, unstriped(n4)]
    pb = h2[:, unstriped(n5)]
    rb = np.minimum(pa, pb)
    ra = np.maximum(pa, pb)
    ua = np.zeros((H, S))
    ua[:, unstriped(n4)] = ra
    ub = ua.copy()
    ub[:, unstriped(n5)] = rb
    return ub - ub[:, unstriped(n6)]

@@ -1,0 +1,246 @@
+from contextlib import ExitStack
+
+import concourse.mybir as mybir
+
+K, T, S, H, G, W = 512, 1024, 256, 512, 2048, 128
+FLOPS = 5 * 2 * K * H * S
+
+F32 = mybir.dt.float32
+BF16 = mybir.dt.bfloat16
+I32 = mybir.dt.int32
+U32 = mybir.dt.uint32
+U16 = mybir.dt.uint16
+U8 = mybir.dt.uint8
+FP8X4 = mybir.dt.float8_e4m3fn_x4
+ACT = mybir.ActivationFunctionType
+ALU = mybir.AluOpType
+
+P = 128
+PACK = 4
+QUAD = 32
+BLOCK_ROWS = 8
+TILES = H // P
+HALF = S // 2
+WIDE = 384
+
+
+def tile_picked_dthzmthesntwordd_none_p_kernel(
+    tc, x_words, x_scales, w1_words, w1_scales, w2_words, w2_scales, sl, th, gs, d_words, d_scales,
+    offs, hz, n1, n2, n3, k1, k2, two, k3, hy, n4, n5, n6, out,
+):
+    nc = tc.nc
+    with ExitStack() as ctx:
+        lists = ctx.enter_context(tc.tile_pool(name="lists", bufs=1))
+        keep = ctx.enter_context(tc.tile_pool(name="keep", bufs=1))
+        psum = ctx.enter_context(tc.psum_pool(name="psum", bufs=1))
+
+        def sbuf(name, shape, dtype, tag=""):
+            return keep.tile(shape, dtype, name=name, tag=tag, align_bytes=64)
+
+        def load_list(name, source):
+            tile = lists.tile(list(source.shape), U16, name=name)
+            nc.sync.dma_start(tile[:], source)
+            return tile
+
+        def load_words(name, source, tag=""):
+            tile = sbuf(name, [P, source.shape[2]], U32, tag)
+            nc.sync.dma_start(tile[:].bitcast(I32), source[0].rearrange("p n r -> p (n r)").bitcast(I32))
+            return tile
+
+        def zeroed_bytes(name, columns):
+            tile = sbuf(name, [P, columns], U8)
+            nc.vector.memset(tile[:].bitcast(I32), 0)
+            return tile
+
+        def gather_words(name, table, offsets):
+            tile = sbuf(name, [P, 16 * offsets.shape[1]], U32)
+            nc.vector.tensor_copy(tile[:], table[:].indirect(offsets[:]))
+            return tile
+
+        def rows_to_places(queue, placed, gathered):
+            for i in range(PACK):
+                queue.dma_start(placed[i:P:QUAD, :].bitcast(I32), gathered[BLOCK_ROWS * i : P : QUAD, :].bitcast(I32))
+
+        def load_rows(target, scales):
+            rows = scales[0].bitcast(I32)
+            nc.sync.dma_start(
+                target.bitcast(I32), rows.unsqueeze(1).broadcast_to([rows.shape[0], BLOCK_ROWS, rows.shape[1]])
+            )
+
+        first_scales = zeroed_bytes("first_scales", 2 * S)
+        second_scales = zeroed_bytes("second_scales", 2 * S + 3 * H)
+
+        hz_list = load_list("hz_list", hz)
+        x_bytes = sbuf("x_bytes", [P, T], U8)
+        load_rows(x_bytes[:], x_scales)
+        offs_list = load_list("offs_list", offs)
+        w_bytes = sbuf("w_bytes", [P, 2 * H], U8)
+        load_rows(w_bytes[:, 0:H], w1_scales)
+        load_rows(w_bytes[:, H : 2 * H], w2_scales)
+        x_table = load_words("x_table", x_words)
+        w1_raw = load_words("w1_raw", w1_words)
+        w2_raw = load_words("w2_raw", w2_words)
+
+        first_gathered = sbuf("first_gathered", [P, 2 * S], U8, "then_dictionary")
+        nc.vector.tensor_copy(first_gathered[:, 0:S], x_bytes[:].indirect(hz_list[:]))
+        nc.vector.tensor_copy(first_gathered[:, S : 2 * S], x_bytes[:].indirect(offs_list[:]))
+        rows_to_places(nc.sync, first_scales, first_gathered)
+
+        w_scales = sbuf("w_scales", [P, 2 * H], U8)
+        nc.vector.tensor_copy(
+            w_scales[:].rearrange("p (a t m) -> p a m t", a=2, t=PACK),
+            w_bytes[:].rearrange("p (a m t) -> p a m t", a=2, t=PACK),
+        )
+        for i in range(1, PACK):
+            nc.sync.dma_start(w_scales[i:P:QUAD, :].bitcast(I32), w_scales[BLOCK_ROWS * i : P : QUAD, :].bitcast(I32))
+        x_offs = gather_words("x_offs", x_table, offs_list)
+        x_hz = gather_words("x_hz", x_table, hz_list)
+
+        n1_list = load_list("n1_list", n1)
+        d_bytes = sbuf("d_bytes", [P, G], U8)
+        load_rows(d_bytes[:], d_scales)
+        n2_list = load_list("n2_list", n2)
+        two_list = load_list("two_list", two)
+        hy_list = load_list("hy_list", hy)
+        k2_list = load_list("k2_list", k2)
+        k3_list = load_list("k3_list", k3)
+        k1_list = load_list("k1_list", k1)
+        d_table = load_words("d_table", d_words, "then_dictionary")
+        n3_list = load_list("n3_list", n3)
+        slope = sbuf("slope", [P, PACK], F32)
+        threshold = sbuf("threshold", [P, PACK], F32)
+        gain = sbuf("gain", [P, PACK], F32)
+        for tile, source in ((slope, sl), (threshold, th), (gain, gs)):
+            nc.sync.dma_start(tile[:], source.rearrange("(p t) o -> p (t o)", t=PACK))
+        n4_list = load_list("n4_list", n4)
+        n5_list = load_list("n5_list", n5)
+        n6_list = load_list("n6_list", n6)
+
+        w1_codes = sbuf("w1_codes", [P, H], U32)
+        w2_codes = sbuf("w2_codes", [P, H], U32)
+        for codes, raw in ((w1_codes, w1_raw), (w2_codes, w2_raw)):
+            nc.scalar.copy(codes[:].rearrange("p (t m) -> p m t", t=PACK), raw[:].rearrange("p (m t) -> p m t", t=PACK))
+
+        y = []
+        for t in range(TILES):
+            rows = slice(P * t, P * (t + 1))
+            bank = psum.tile([P, S], F32, name=f"y_bank{t}")
+            nc.tensor.matmul_mx(
+                bank[:], lhsT=w1_codes[:, rows].bitcast(FP8X4), lhsT_scale=w_scales[:, rows],
+                rhs=x_offs[:].bitcast(FP8X4), rhs_scale=first_scales[:, S : 2 * S], start=True, stop=False,
+            )
+            nc.tensor.matmul_mx(
+                bank[:], lhsT=w2_codes[:, rows].bitcast(FP8X4), lhsT_scale=w_scales[:, H + P * t : H + P * (t + 1)],
+                rhs=x_hz[:].bitcast(FP8X4), rhs_scale=first_scales[:, 0:S], start=False, stop=True,
+            )
+            y_tile = sbuf(f"y{t}", [P, S], F32)
+            if t == 0:
+                nc.scalar.copy(y_tile[:], bank[:])
+            else:
+                nc.vector.tensor_copy(y_tile[:], bank[:])
+            y.append(y_tile)
+
+        ds = [sbuf(f"ds{t}", [P, WIDE], F32) for t in range(TILES)]
+        ds2 = [sbuf(f"ds2_{t}", [P, WIDE], F32) for t in range(TILES)]
+        for t in range(TILES):
+            nc.scalar.activation(ds[t][:].indirect(n1_list[:]), y[t][:], ACT.Copy)
+            nc.scalar.activation(ds2[t][:].indirect(n2_list[:]), y[t][:], ACT.Copy)
+
+        second_gathered = sbuf("second_gathered", [P, 2 * S + 3 * H], U8)
+        column = 0
+        place = {}
+        for name, table, offsets in (
+            ("two", x_bytes, two_list), ("hy", x_bytes, hy_list),
+            ("k2", d_bytes, k2_list), ("k3", d_bytes, k3_list), ("k1", d_bytes, k1_list),
+        ):
+            width = 16 * offsets.shape[1]
+            nc.vector.tensor_copy(second_gathered[:, column : column + width], table[:].indirect(offsets[:]))
+            place[name] = column
+            column = column + width
+        rows_to_places(nc.sync, second_scales, second_gathered)
+        x_two = gather_words("x_two", x_table, two_list)
+        d_k2 = gather_words("d_k2", d_table, k2_list)
+        x_hy = gather_words("x_hy", x_table, hy_list)
+        d_k3 = gather_words("d_k3", d_table, k3_list)
+        d_k1 = gather_words("d_k1", d_table, k1_list)
+
+        h_banks = [psum.tile([P, S], F32, name=f"h_bank{t}") for t in range(TILES)]
+
+        def second_pass(t, columns, codes, name, moving, moving_scales, start, stop):
+            nc.tensor.matmul_mx(
+                h_banks[t][:, columns], lhsT=codes[:, P * t : P * (t + 1)].bitcast(FP8X4),
+                lhsT_scale=second_scales[:, place[name] + P * t : place[name] + P * (t + 1)],
+                rhs=moving.bitcast(FP8X4), rhs_scale=moving_scales, start=start, stop=stop,
+            )
+
+        for t in range(TILES):
+            second_pass(t, slice(0, S), d_k2, "k2", x_two[:], second_scales[:, place["two"] : place["two"] + S], True, False)
+        for t in range(TILES):
+            second_pass(t, slice(0, S), d_k3, "k3", x_hy[:], second_scales[:, place["hy"] : place["hy"] + S], False, False)
+
+        bias = sbuf("bias", [P, PACK], F32)
+        nc.vector.scalar_tensor_tensor(bias[:], slope[:], -1.0, threshold[:], ALU.mult, ALU.mult)
+        weighted = sbuf("weighted", [P, TILES, S], F32)
+        for t in range(TILES):
+            nc.vector.tensor_scalar(weighted[:, t, :], ds2[t][:, 0:S], gain[:, t : t + 1], None, ALU.mult)
+
+        for half in range(2):
+            columns = slice(HALF * half, HALF * (half + 1))
+            sg = sbuf(f"sg{half}", [P, TILES, HALF], F32)
+            for t in range(TILES):
+                nc.scalar.activation(
+                    sg[:, t, :], ds[t][:].indirect(n3_list[:, HALF // 16 * half : HALF // 16 * (half + 1)]), ACT.Sigmoid,
+                    bias=bias[:, t : t + 1], scale=slope[:, t : t + 1],
+                )
+            z = sbuf(f"z{half}", [P, HALF * PACK], BF16)
+            nc.vector.tensor_tensor(
+                z[:].rearrange("p (c i t) -> p c t i", i=4, t=PACK),
+                weighted[:, :, columns].rearrange("p t (c i) -> p c t i", i=4),
+                sg[:].rearrange("p t (c i) -> p c t i", i=4),
+                ALU.mult,
+            )
+            z_codes = sbuf(f"z_codes{half}", [P, HALF], U32)
+            z_scales = sbuf(f"z_scales{half}", [P, HALF], U8)
+            nc.vector.quantize_mx(z_codes[:].bitcast(FP8X4), z_scales[:], z[:])
+            for t in range(TILES):
+                second_pass(t, columns, d_k1, "k1", z_codes[:], z_scales[:], False, half == 1)
+
+        h2 = [sbuf(f"h2_{t}", [P, S], F32) for t in range(TILES)]
+        ub = [sbuf(f"ub{t}", [P, WIDE], F32) for t in range(TILES)]
+        larger = [sbuf(f"larger{t}", [P, W], F32) for t in range(TILES)]
+        smaller = [sbuf(f"smaller{t}", [P, W], F32) for t in range(TILES)]
+
+        def fetch_pairs(t):
+            nc.vector.tensor_scalar(h2[t][:], h_banks[t][:], 0.0625, None, ALU.mult)
+            pa = sbuf(f"pa{t}", [P, W], F32)
+            pb = sbuf(f"pb{t}", [P, W], F32)
+            nc.scalar.activation(pa[:], h2[t][:].indirect(n4_list[:]), ACT.Copy)
+            nc.scalar.activation(pb[:], h2[t][:].indirect(n5_list[:]), ACT.Copy)
+            nc.vector.tensor_tensor(larger[t][:], pa[:], pb[:], ALU.max)
+            nc.vector.tensor_tensor(smaller[t][:], pa[:], pb[:], ALU.min)
+
+        def put_larger(t):
+            nc.scalar.activation(ub[t][:].indirect(n4_list[:]), larger[t][:], ACT.Copy)
+
+        def put_smaller(t):
+            nc.scalar.activation(ub[t][:].indirect(n5_list[:]), smaller[t][:], ACT.Copy)
+
+        def finish(t):
+            width = HALF if t == TILES - 1 else S
+            for start in range(0, S, width):
+                columns = slice(start, start + width)
+                fetched = sbuf(f"fetched{t}_{start}", [P, width], F32)
+                nc.scalar.activation(fetched[:], ub[t][:].indirect(n6_list[:, start // 16 : (start + width) // 16]), ACT.Copy)
+                result = sbuf(f"result{t}_{start}", [P, width], F32)
+                nc.vector.tensor_tensor(result[:], ub[t][:, columns], fetched[:], ALU.subtract)
+                nc.sync.dma_start(out[P * t : P * (t + 1), columns], result[:])
+
+        for t in range(TILES):
+            fetch_pairs(t)
+        for pair in range(0, TILES, 2):
+            put_larger(pair)
+            put_larger(pair + 1)
+            put_smaller(pair)
+            put_smaller(pair + 1)
+            finish(pair)
+            finish(pair + 1)

@@ -67,6 +67,11 @@ def tile_picked_dthzmthesntwordd_none_p_kernel(
                 target.bitcast(I32), rows.unsqueeze(1).broadcast_to([rows.shape[0], BLOCK_ROWS, rows.shape[1]])
             )
 
+        warm_in = sbuf("warm_in", [P, 1], F32)
+        warm_out = sbuf("warm_out", [P, 1], F32)
+        nc.gpsimd.memset(warm_in[:], 0.0)
+        nc.scalar.activation(warm_out[:], warm_in[:], ACT.Sigmoid)
+
         first_scales = zeroed_bytes("first_scales", 2 * S)
         second_scales = zeroed_bytes("second_scales", 2 * S + 3 * H)
 

@@ -22,6 +22,7 @@ BLOCK_ROWS = 8
 TILES = H // P
 HALF = S // 2
 WIDE = 384
+EARLY_TILES = 2
 
 
 def tile_picked_dthzmthesntwordd_none_p_kernel(
@@ -57,54 +58,72 @@ def tile_picked_dthzmthesntwordd_none_p_kernel(
             nc.vector.tensor_copy(tile[:], table[:].indirect(offsets[:]))
             return tile
 
-        def rows_to_places(queue, placed, gathered):
-            for i in range(PACK):
-                queue.dma_start(placed[i:P:QUAD, :].bitcast(I32), gathered[BLOCK_ROWS * i : P : QUAD, :].bitcast(I32))
+        def rows_to_places(placed, gathered, first):
+            for i in range(first, PACK):
+                nc.sync.dma_start(placed[i:P:QUAD, :].bitcast(I32), gathered[BLOCK_ROWS * i : P : QUAD, :].bitcast(I32))
 
-        def load_rows(target, scales):
+        def load_rows(name, scales):
             rows = scales[0].bitcast(I32)
+            tile = sbuf(name, [P, scales.shape[2]], U8)
             nc.sync.dma_start(
-                target.bitcast(I32), rows.unsqueeze(1).broadcast_to([rows.shape[0], BLOCK_ROWS, rows.shape[1]])
+                tile[:].bitcast(I32), rows.unsqueeze(1).broadcast_to([rows.shape[0], BLOCK_ROWS, rows.shape[1]])
             )
+            return tile
 
+        halves = [slice(0, HALF), slice(HALF, S)]
+
+        def entries(offsets, columns):
+            return offsets[:, columns.start // 16 : columns.stop // 16]
+
+        w_bytes = sbuf("w_bytes", [P, 2 * H], U8, "then_late_words")
+        nc.gpsimd.memset(w_bytes[:].bitcast(I32), 0)
         warm_in = sbuf("warm_in", [P, 1], F32)
         warm_out = sbuf("warm_out", [P, 1], F32)
         nc.gpsimd.memset(warm_in[:], 0.0)
         nc.scalar.activation(warm_out[:], warm_in[:], ACT.Sigmoid)
 
-        first_scales = zeroed_bytes("first_scales", 2 * S)
         second_scales = zeroed_bytes("second_scales", 2 * S + 3 * H)
 
         hz_list = load_list("hz_list", hz)
-        x_bytes = sbuf("x_bytes", [P, T], U8)
-        load_rows(x_bytes[:], x_scales)
+        x_bytes = load_rows("x_bytes", x_scales)
+        for a, scales in enumerate((w1_scales, w2_scales)):
+            nc.sync.dma_start(w_bytes[0:P:BLOCK_ROWS, H * a : H * (a + 1)].bitcast(I32), scales[0].bitcast(I32))
         offs_list = load_list("offs_list", offs)
-        w_bytes = sbuf("w_bytes", [P, 2 * H], U8)
-        load_rows(w_bytes[:, 0:H], w1_scales)
-        load_rows(w_bytes[:, H : 2 * H], w2_scales)
-        x_table = load_words("x_table", x_words)
         w1_raw = load_words("w1_raw", w1_words)
         w2_raw = load_words("w2_raw", w2_words)
+        x_table = load_words("x_table", x_words)
+        rows_to_places(w_bytes, w_bytes, 1)
 
-        first_gathered = sbuf("first_gathered", [P, 2 * S], U8, "then_dictionary")
-        nc.vector.tensor_copy(first_gathered[:, 0:S], x_bytes[:].indirect(hz_list[:]))
-        nc.vector.tensor_copy(first_gathered[:, S : 2 * S], x_bytes[:].indirect(offs_list[:]))
-        rows_to_places(nc.sync, first_scales, first_gathered)
+        def first_scales(half, tag):
+            gathered = sbuf(f"first_gathered{half}", [P, S], U8, tag)
+            nc.vector.tensor_copy(gathered[:, 0:HALF], x_bytes[:].indirect(entries(hz_list, halves[half])))
+            nc.vector.tensor_copy(gathered[:, HALF:S], x_bytes[:].indirect(entries(offs_list, halves[half])))
+            placed = sbuf(f"first_scales{half}", [P, S], U8)
+            nc.vector.tensor_copy(placed[:].bitcast(I32), gathered[:].bitcast(I32))
+            rows_to_places(placed, gathered, 1)
+            return placed
+
+        def first_words(half, tag):
+            words = sbuf(f"first_words{half}", [P, S], U32, tag)
+            nc.vector.tensor_copy(words[:, 0:HALF], x_table[:].indirect(entries(hz_list, halves[half])))
+            nc.vector.tensor_copy(words[:, HALF:S], x_table[:].indirect(entries(offs_list, halves[half])))
+            return words
+
+        x_scale_halves = [first_scales(0, "")]
+        n1_list = load_list("n1_list", n1)
+        x_scale_halves.append(first_scales(1, "then_dictionary"))
+        x_word_halves = [first_words(0, "")]
 
         w_scales = sbuf("w_scales", [P, 2 * H], U8)
-        nc.vector.tensor_copy(
-            w_scales[:].rearrange("p (a t m) -> p a m t", a=2, t=PACK),
-            w_bytes[:].rearrange("p (a m t) -> p a m t", a=2, t=PACK),
-        )
-        for i in range(1, PACK):
-            nc.sync.dma_start(w_scales[i:P:QUAD, :].bitcast(I32), w_scales[BLOCK_ROWS * i : P : QUAD, :].bitcast(I32))
-        x_offs = gather_words("x_offs", x_table, offs_list)
-        x_hz = gather_words("x_hz", x_table, hz_list)
+        for tiles in (slice(0, 1), slice(1, TILES)):
+            nc.vector.tensor_copy(
+                w_scales[:].rearrange("p (a t m) -> p a m t", a=2, t=PACK)[:, :, :, tiles],
+                w_bytes[:].rearrange("p (a m t) -> p a m t", a=2, t=PACK)[:, :, :, tiles],
+            )
+        x_word_halves.append(first_words(1, "then_late_words"))
 
-        n1_list = load_list("n1_list", n1)
-        d_bytes = sbuf("d_bytes", [P, G], U8)
-        load_rows(d_bytes[:], d_scales)
         n2_list = load_list("n2_list", n2)
+        d_bytes = load_rows("d_bytes", d_scales)
         two_list = load_list("two_list", two)
         hy_list = load_list("hy_list", hy)
         k2_list = load_list("k2_list", k2)
@@ -126,29 +145,36 @@ def tile_picked_dthzmthesntwordd_none_p_kernel(
         for codes, raw in ((w1_codes, w1_raw), (w2_codes, w2_raw)):
             nc.scalar.copy(codes[:].rearrange("p (t m) -> p m t", t=PACK), raw[:].rearrange("p (m t) -> p m t", t=PACK))
 
-        y = []
-        for t in range(TILES):
-            rows = slice(P * t, P * (t + 1))
-            bank = psum.tile([P, S], F32, name=f"y_bank{t}")
-            nc.tensor.matmul_mx(
-                bank[:], lhsT=w1_codes[:, rows].bitcast(FP8X4), lhsT_scale=w_scales[:, rows],
-                rhs=x_offs[:].bitcast(FP8X4), rhs_scale=first_scales[:, S : 2 * S], start=True, stop=False,
-            )
-            nc.tensor.matmul_mx(
-                bank[:], lhsT=w2_codes[:, rows].bitcast(FP8X4), lhsT_scale=w_scales[:, H + P * t : H + P * (t + 1)],
-                rhs=x_hz[:].bitcast(FP8X4), rhs_scale=first_scales[:, 0:S], start=False, stop=True,
-            )
-            y_tile = sbuf(f"y{t}", [P, S], F32)
-            if t == 0:
-                nc.scalar.copy(y_tile[:], bank[:])
-            else:
-                nc.vector.tensor_copy(y_tile[:], bank[:])
-            y.append(y_tile)
+        y = [sbuf(f"y{t}", [P, S], F32) for t in range(TILES)]
+        y_banks = [psum.tile([P, S], F32, name=f"y_bank{t}", tag=f"first{t}") for t in range(TILES)]
+        for half, columns in enumerate(halves):
+            words, scales = x_word_halves[half], x_scale_halves[half]
+            for t in range(TILES):
+                rows = slice(P * t, P * (t + 1))
+                nc.tensor.matmul_mx(
+                    y_banks[t][:, columns], lhsT=w1_codes[:, rows].bitcast(FP8X4), lhsT_scale=w_scales[:, rows],
+                    rhs=words[:, HALF:S].bitcast(FP8X4), rhs_scale=scales[:, HALF:S], start=True, stop=False,
+                )
+                nc.tensor.matmul_mx(
+                    y_banks[t][:, columns], lhsT=w2_codes[:, rows].bitcast(FP8X4),
+                    lhsT_scale=w_scales[:, H + P * t : H + P * (t + 1)],
+                    rhs=words[:, 0:HALF].bitcast(FP8X4), rhs_scale=scales[:, 0:HALF], start=False, stop=True,
+                )
+                if t == 0 and half == 0:
+                    nc.scalar.copy(y[t][:, columns], y_banks[t][:, columns])
+                elif t < EARLY_TILES:
+                    nc.vector.tensor_copy(y[t][:, columns], y_banks[t][:, columns])
+                elif half == 1:
+                    nc.vector.tensor_copy(y[t][:], y_banks[t][:])
 
         ds = [sbuf(f"ds{t}", [P, WIDE], F32) for t in range(TILES)]
         ds2 = [sbuf(f"ds2_{t}", [P, WIDE], F32) for t in range(TILES)]
+        for columns in halves:
+            for t in range(EARLY_TILES):
+                nc.scalar.activation(ds[t][:].indirect(entries(n1_list, columns)), y[t][:, columns], ACT.Copy)
         for t in range(TILES):
-            nc.scalar.activation(ds[t][:].indirect(n1_list[:]), y[t][:], ACT.Copy)
+            if t >= EARLY_TILES:
+                nc.scalar.activation(ds[t][:].indirect(n1_list[:]), y[t][:], ACT.Copy)
             nc.scalar.activation(ds2[t][:].indirect(n2_list[:]), y[t][:], ACT.Copy)
 
         second_gathered = sbuf("second_gathered", [P, 2 * S + 3 * H], U8)
@@ -162,7 +188,7 @@ def tile_picked_dthzmthesntwordd_none_p_kernel(
             nc.vector.tensor_copy(second_gathered[:, column : column + width], table[:].indirect(offsets[:]))
             place[name] = column
             column = column + width
-        rows_to_places(nc.sync, second_scales, second_gathered)
+        rows_to_places(second_scales, second_gathered, 0)
         x_two = gather_words("x_two", x_table, two_list)
         d_k2 = gather_words("d_k2", d_table, k2_list)
         x_hy = gather_words("x_hy", x_table, hy_list)
@@ -170,53 +196,61 @@ def tile_picked_dthzmthesntwordd_none_p_kernel(
         d_k1 = gather_words("d_k1", d_table, k1_list)
 
         h_banks = [psum.tile([P, S], F32, name=f"h_bank{t}") for t in range(TILES)]
+        early_bank = psum.tile([P, S], F32, name="early_bank", tag="first0")
 
         def second_pass(t, columns, codes, name, moving, moving_scales, start, stop):
+            bank = early_bank if (t == 0 and columns == halves[0]) else h_banks[t]
             nc.tensor.matmul_mx(
-                h_banks[t][:, columns], lhsT=codes[:, P * t : P * (t + 1)].bitcast(FP8X4),
+                bank[:, columns], lhsT=codes[:, P * t : P * (t + 1)].bitcast(FP8X4),
                 lhsT_scale=second_scales[:, place[name] + P * t : place[name] + P * (t + 1)],
                 rhs=moving.bitcast(FP8X4), rhs_scale=moving_scales, start=start, stop=stop,
             )
 
-        for t in range(TILES):
-            second_pass(t, slice(0, S), d_k2, "k2", x_two[:], second_scales[:, place["two"] : place["two"] + S], True, False)
-        for t in range(TILES):
-            second_pass(t, slice(0, S), d_k3, "k3", x_hy[:], second_scales[:, place["hy"] : place["hy"] + S], False, False)
+        for codes, name, moving, moving_name in ((d_k2, "k2", x_two, "two"), (d_k3, "k3", x_hy, "hy")):
+            for t in range(TILES):
+                for columns in halves if t == 0 else [slice(0, S)]:
+                    scales = second_scales[:, place[moving_name] + columns.start : place[moving_name] + columns.stop]
+                    second_pass(t, columns, codes, name, moving[:, columns], scales, name == "k2", False)
 
+        h2 = [sbuf(f"h2_{t}", [P, S], F32) for t in range(TILES)]
         bias = sbuf("bias", [P, PACK], F32)
         nc.vector.scalar_tensor_tensor(bias[:], slope[:], -1.0, threshold[:], ALU.mult, ALU.mult)
         weighted = sbuf("weighted", [P, TILES, S], F32)
         for t in range(TILES):
             nc.vector.tensor_scalar(weighted[:, t, :], ds2[t][:, 0:S], gain[:, t : t + 1], None, ALU.mult)
 
-        for half in range(2):
-            columns = slice(HALF * half, HALF * (half + 1))
+        for half, columns in enumerate(halves):
             sg = sbuf(f"sg{half}", [P, TILES, HALF], F32)
-            for t in range(TILES):
-                nc.scalar.activation(
-                    sg[:, t, :], ds[t][:].indirect(n3_list[:, HALF // 16 * half : HALF // 16 * (half + 1)]), ACT.Sigmoid,
-                    bias=bias[:, t : t + 1], scale=slope[:, t : t + 1],
-                )
             z = sbuf(f"z{half}", [P, HALF * PACK], BF16)
-            nc.vector.tensor_tensor(
-                z[:].rearrange("p (c i t) -> p c t i", i=4, t=PACK),
-                weighted[:, :, columns].rearrange("p t (c i) -> p c t i", i=4),
-                sg[:].rearrange("p t (c i) -> p c t i", i=4),
-                ALU.mult,
-            )
+            step = TILES if half == 0 else TILES // 2
+            for first in range(0, TILES, step):
+                group = slice(first, first + step)
+                for t in range(first, first + step):
+                    nc.scalar.activation(
+                        sg[:, t, :], ds[t][:].indirect(n3_list[:, columns.start // 16 : columns.stop // 16]), ACT.Sigmoid,
+                        bias=bias[:, t : t + 1], scale=slope[:, t : t + 1],
+                    )
+                nc.vector.tensor_tensor(
+                    z[:].rearrange("p (c i t) -> p c t i", i=4, t=PACK)[:, :, group, :],
+                    weighted[:, group, columns].rearrange("p t (c i) -> p c t i", i=4),
+                    sg[:, group, :].rearrange("p t (c i) -> p c t i", i=4),
+                    ALU.mult,
+                )
             z_codes = sbuf(f"z_codes{half}", [P, HALF], U32)
             z_scales = sbuf(f"z_scales{half}", [P, HALF], U8)
             nc.vector.quantize_mx(z_codes[:].bitcast(FP8X4), z_scales[:], z[:])
             for t in range(TILES):
-                second_pass(t, columns, d_k1, "k1", z_codes[:], z_scales[:], False, half == 1)
+                second_pass(t, columns, d_k1, "k1", z_codes[:], z_scales[:], False, half == 1 or t == 0)
+            if half == 0:
+                nc.vector.tensor_scalar(h2[0][:, columns], early_bank[:, columns], 0.0625, None, ALU.mult)
 
-        h2 = [sbuf(f"h2_{t}", [P, S], F32) for t in range(TILES)]
         ub = [sbuf(f"ub{t}", [P, WIDE], F32) for t in range(TILES)]
         larger = [sbuf(f"larger{t}", [P, W], F32) for t in range(TILES)]
         smaller = [sbuf(f"smaller{t}", [P, W], F32) for t in range(TILES)]
 
         def fetch_pairs(t):
-            nc.vector.tensor_scalar(h2[t][:], h_banks[t][:], 0.0625, None, ALU.mult)
+            columns = halves[1] if t == 0 else slice(0, S)
+            nc.vector.tensor_scalar(h2[t][:, columns], h_banks[t][:, columns], 0.0625, None, ALU.mult)
             pa = sbuf(f"pa{t}", [P, W], F32)
             pb = sbuf(f"pb{t}", [P, W], F32)
             nc.scalar.activation(pa[:], h2[t][:].indirect(n4_list[:]), ACT.Copy)

@@ -75,7 +75,7 @@ def tile_picked_dthzmthesntwordd_none_p_kernel(
         def entries(offsets, columns):
             return offsets[:, columns.start // 16 : columns.stop // 16]
 
-        w_bytes = sbuf("w_bytes", [P, 2 * H], U8, "then_late_words")
+        w_bytes = sbuf("w_bytes", [P, 2 * H], U8)
         nc.gpsimd.memset(w_bytes[:].bitcast(I32), 0)
         warm_in = sbuf("warm_in", [P, 1], F32)
         warm_out = sbuf("warm_out", [P, 1], F32)
@@ -89,9 +89,9 @@ def tile_picked_dthzmthesntwordd_none_p_kernel(
         for a, scales in enumerate((w1_scales, w2_scales)):
             nc.sync.dma_start(w_bytes[0:P:BLOCK_ROWS, H * a : H * (a + 1)].bitcast(I32), scales[0].bitcast(I32))
         offs_list = load_list("offs_list", offs)
+        x_table = load_words("x_table", x_words)
         w1_raw = load_words("w1_raw", w1_words)
         w2_raw = load_words("w2_raw", w2_words)
-        x_table = load_words("x_table", x_words)
         rows_to_places(w_bytes, w_bytes, 1)
 
         def first_scales(half, tag):
@@ -103,8 +103,8 @@ def tile_picked_dthzmthesntwordd_none_p_kernel(
             rows_to_places(placed, gathered, 1)
             return placed
 
-        def first_words(half, tag):
-            words = sbuf(f"first_words{half}", [P, S], U32, tag)
+        def first_words(half):
+            words = sbuf(f"first_words{half}", [P, S], U32)
             nc.vector.tensor_copy(words[:, 0:HALF], x_table[:].indirect(entries(hz_list, halves[half])))
             nc.vector.tensor_copy(words[:, HALF:S], x_table[:].indirect(entries(offs_list, halves[half])))
             return words
@@ -112,7 +112,7 @@ def tile_picked_dthzmthesntwordd_none_p_kernel(
         x_scale_halves = [first_scales(0, "")]
         n1_list = load_list("n1_list", n1)
         x_scale_halves.append(first_scales(1, "then_dictionary"))
-        x_word_halves = [first_words(0, "")]
+        x_word_halves = [first_words(0), first_words(1)]
 
         w_scales = sbuf("w_scales", [P, 2 * H], U8)
         for tiles in (slice(0, 1), slice(1, TILES)):
@@ -120,7 +120,6 @@ def tile_picked_dthzmthesntwordd_none_p_kernel(
                 w_scales[:].rearrange("p (a t m) -> p a m t", a=2, t=PACK)[:, :, :, tiles],
                 w_bytes[:].rearrange("p (a m t) -> p a m t", a=2, t=PACK)[:, :, :, tiles],
             )
-        x_word_halves.append(first_words(1, "then_late_words"))
 
         n2_list = load_list("n2_list", n2)
         d_bytes = load_rows("d_bytes", d_scales)
@@ -143,7 +142,11 @@ def tile_picked_dthzmthesntwordd_none_p_kernel(
         w1_codes = sbuf("w1_codes", [P, H], U32)
         w2_codes = sbuf("w2_codes", [P, H], U32)
         for codes, raw in ((w1_codes, w1_raw), (w2_codes, w2_raw)):
-            nc.scalar.copy(codes[:].rearrange("p (t m) -> p m t", t=PACK), raw[:].rearrange("p (m t) -> p m t", t=PACK))
+            for tiles in (slice(0, 1), slice(1, TILES)):
+                nc.scalar.copy(
+                    codes[:].rearrange("p (t m) -> p m t", t=PACK)[:, :, tiles],
+                    raw[:].rearrange("p (m t) -> p m t", t=PACK)[:, :, tiles],
+                )
 
         y = [sbuf(f"y{t}", [P, S], F32) for t in range(TILES)]
         y_banks = [psum.tile([P, S], F32, name=f"y_bank{t}", tag=f"first{t}") for t in range(TILES)]
@@ -222,7 +225,7 @@ def tile_picked_dthzmthesntwordd_none_p_kernel(
         for half, columns in enumerate(halves):
             sg = sbuf(f"sg{half}", [P, TILES, HALF], F32)
             z = sbuf(f"z{half}", [P, HALF * PACK], BF16)
-            step = TILES if half == 0 else TILES // 2
+            step = TILES // 2
             for first in range(0, TILES, step):
                 group = slice(first, first + step)
                 for t in range(first, first + step):

from contextlib import ExitStack

import concourse.mybir as mybir

K, T, S, H, G, W = 512, 1024, 256, 512, 2048, 128
FLOPS = 5 * 2 * K * H * S

F32 = mybir.dt.float32
BF16 = mybir.dt.bfloat16
I32 = mybir.dt.int32
U32 = mybir.dt.uint32
U16 = mybir.dt.uint16
U8 = mybir.dt.uint8
FP8X4 = mybir.dt.float8_e4m3fn_x4
ACT = mybir.ActivationFunctionType
ALU = mybir.AluOpType

P = 128
PACK = 4
QUAD = 32
BLOCK_ROWS = 8
TILES = H // P
HALF = S // 2
WIDE = 384
EARLY_TILES = 2


def tile_picked_dthzmthesntwordd_none_p_kernel(
    tc, x_words, x_scales, w1_words, w1_scales, w2_words, w2_scales, sl, th, gs, d_words, d_scales,
    offs, hz, n1, n2, n3, k1, k2, two, k3, hy, n4, n5, n6, out,
):
    nc = tc.nc
    with ExitStack() as ctx:
        lists = ctx.enter_context(tc.tile_pool(name="lists", bufs=1))
        keep = ctx.enter_context(tc.tile_pool(name="keep", bufs=1))
        psum = ctx.enter_context(tc.psum_pool(name="psum", bufs=1))

        def sbuf(name, shape, dtype, tag=""):
            return keep.tile(shape, dtype, name=name, tag=tag, align_bytes=64)

        def load_list(name, source):
            tile = lists.tile(list(source.shape), U16, name=name)
            nc.sync.dma_start(tile[:], source)
            return tile

        def load_words(name, source, tag=""):
            tile = sbuf(name, [P, source.shape[2]], U32, tag)
            nc.sync.dma_start(tile[:].bitcast(I32), source[0].rearrange("p n r -> p (n r)").bitcast(I32))
            return tile

        def zeroed_bytes(name, columns):
            tile = sbuf(name, [P, columns], U8)
            nc.vector.memset(tile[:].bitcast(I32), 0)
            return tile

        def gather_words(name, table, offsets):
            tile = sbuf(name, [P, 16 * offsets.shape[1]], U32)
            nc.vector.tensor_copy(tile[:], table[:].indirect(offsets[:]))
            return tile

        def rows_to_places(placed, gathered, first):
            for i in range(first, PACK):
                nc.sync.dma_start(placed[i:P:QUAD, :].bitcast(I32), gathered[BLOCK_ROWS * i : P : QUAD, :].bitcast(I32))

        def load_rows(name, scales):
            rows = scales[0].bitcast(I32)
            tile = sbuf(name, [P, scales.shape[2]], U8)
            nc.sync.dma_start(
                tile[:].bitcast(I32), rows.unsqueeze(1).broadcast_to([rows.shape[0], BLOCK_ROWS, rows.shape[1]])
            )
            return tile

        halves = [slice(0, HALF), slice(HALF, S)]

        def entries(offsets, columns):
            return offsets[:, columns.start // 16 : columns.stop // 16]

        w_bytes = sbuf("w_bytes", [P, 2 * H], U8)
        nc.gpsimd.memset(w_bytes[:].bitcast(I32), 0)
        warm_in = sbuf("warm_in", [P, 1], F32)
        warm_out = sbuf("warm_out", [P, 1], F32)
        nc.gpsimd.memset(warm_in[:], 0.0)
        nc.scalar.activation(warm_out[:], warm_in[:], ACT.Sigmoid)

        second_scales = zeroed_bytes("second_scales", 2 * S + 3 * H)

        hz_list = load_list("hz_list", hz)
        x_bytes = load_rows("x_bytes", x_scales)
        for a, scales in enumerate((w1_scales, w2_scales)):
            nc.sync.dma_start(w_bytes[0:P:BLOCK_ROWS, H * a : H * (a + 1)].bitcast(I32), scales[0].bitcast(I32))
        offs_list = load_list("offs_list", offs)
        x_table = load_words("x_table", x_words)
        w1_raw = load_words("w1_raw", w1_words)
        w2_raw = load_words("w2_raw", w2_words)
        rows_to_places(w_bytes, w_bytes, 1)

        def first_scales(half, tag):
            gathered = sbuf(f"first_gathered{half}", [P, S], U8, tag)
            nc.vector.tensor_copy(gathered[:, 0:HALF], x_bytes[:].indirect(entries(hz_list, halves[half])))
            nc.vector.tensor_copy(gathered[:, HALF:S], x_bytes[:].indirect(entries(offs_list, halves[half])))
            placed = sbuf(f"first_scales{half}", [P, S], U8)
            nc.vector.tensor_copy(placed[:].bitcast(I32), gathered[:].bitcast(I32))
            rows_to_places(placed, gathered, 1)
            return placed

        def first_words(half):
            words = sbuf(f"first_words{half}", [P, S], U32)
            nc.vector.tensor_copy(words[:, 0:HALF], x_table[:].indirect(entries(hz_list, halves[half])))
            nc.vector.tensor_copy(words[:, HALF:S], x_table[:].indirect(entries(offs_list, halves[half])))
            return words

        x_scale_halves = [first_scales(0, "")]
        n1_list = load_list("n1_list", n1)
        x_scale_halves.append(first_scales(1, "then_dictionary"))
        x_word_halves = [first_words(0), first_words(1)]

        w_scales = sbuf("w_scales", [P, 2 * H], U8)
        for tiles in (slice(0, 1), slice(1, TILES)):
            nc.vector.tensor_copy(
                w_scales[:].rearrange("p (a t m) -> p a m t", a=2, t=PACK)[:, :, :, tiles],
                w_bytes[:].rearrange("p (a m t) -> p a m t", a=2, t=PACK)[:, :, :, tiles],
            )

        n2_list = load_list("n2_list", n2)
        d_bytes = load_rows("d_bytes", d_scales)
        two_list = load_list("two_list", two)
        hy_list = load_list("hy_list", hy)
        k2_list = load_list("k2_list", k2)
        k3_list = load_list("k3_list", k3)
        k1_list = load_list("k1_list", k1)
        d_table = load_words("d_table", d_words, "then_dictionary")
        n3_list = load_list("n3_list", n3)
        slope = sbuf("slope", [P, PACK], F32)
        threshold = sbuf("threshold", [P, PACK], F32)
        gain = sbuf("gain", [P, PACK], F32)
        for tile, source in ((slope, sl), (threshold, th), (gain, gs)):
            nc.sync.dma_start(tile[:], source.rearrange("(p t) o -> p (t o)", t=PACK))
        n4_list = load_list("n4_list", n4)
        n5_list = load_list("n5_list", n5)
        n6_list = load_list("n6_list", n6)

        w1_codes = sbuf("w1_codes", [P, H], U32)
        w2_codes = sbuf("w2_codes", [P, H], U32)
        for codes, raw in ((w1_codes, w1_raw), (w2_codes, w2_raw)):
            for tiles in (slice(0, 1), slice(1, TILES)):
                nc.scalar.copy(
                    codes[:].rearrange("p (t m) -> p m t", t=PACK)[:, :, tiles],
                    raw[:].rearrange("p (m t) -> p m t", t=PACK)[:, :, tiles],
                )

        y = [sbuf(f"y{t}", [P, S], F32) for t in range(TILES)]
        y_banks = [psum.tile([P, S], F32, name=f"y_bank{t}", tag=f"first{t}") for t in range(TILES)]
        for half, columns in enumerate(halves):
            words, scales = x_word_halves[half], x_scale_halves[half]
            for t in range(TILES):
                rows = slice(P * t, P * (t + 1))
                nc.tensor.matmul_mx(
                    y_banks[t][:, columns], lhsT=w1_codes[:, rows].bitcast(FP8X4), lhsT_scale=w_scales[:, rows],
                    rhs=words[:, HALF:S].bitcast(FP8X4), rhs_scale=scales[:, HALF:S], start=True, stop=False,
                )
                nc.tensor.matmul_mx(
                    y_banks[t][:, columns], lhsT=w2_codes[:, rows].bitcast(FP8X4),
                    lhsT_scale=w_scales[:, H + P * t : H + P * (t + 1)],
                    rhs=words[:, 0:HALF].bitcast(FP8X4), rhs_scale=scales[:, 0:HALF], start=False, stop=True,
                )
                if t == 0 and half == 0:
                    nc.scalar.copy(y[t][:, columns], y_banks[t][:, columns])
                elif t < EARLY_TILES:
                    nc.vector.tensor_copy(y[t][:, columns], y_banks[t][:, columns])
                elif half == 1:
                    nc.vector.tensor_copy(y[t][:], y_banks[t][:])

        ds = [sbuf(f"ds{t}", [P, WIDE], F32) for t in range(TILES)]
        ds2 = [sbuf(f"ds2_{t}", [P, WIDE], F32) for t in range(TILES)]
        for columns in halves:
            for t in range(EARLY_TILES):
                nc.scalar.activation(ds[t][:].indirect(entries(n1_list, columns)), y[t][:, columns], ACT.Copy)
        for t in range(TILES):
            if t >= EARLY_TILES:
                nc.scalar.activation(ds[t][:].indirect(n1_list[:]), y[t][:], ACT.Copy)
            nc.scalar.activation(ds2[t][:].indirect(n2_list[:]), y[t][:], ACT.Copy)

        second_gathered = sbuf("second_gathered", [P, 2 * S + 3 * H], U8)
        column = 0
        place = {}
        for name, table, offsets in (
            ("two", x_bytes, two_list), ("hy", x_bytes, hy_list),
            ("k2", d_bytes, k2_list), ("k3", d_bytes, k3_list), ("k1", d_bytes, k1_list),
        ):
            width = 16 * offsets.shape[1]
            nc.vector.tensor_copy(second_gathered[:, column : column + width], table[:].indirect(offsets[:]))
            place[name] = column
            column = column + width
        rows_to_places(second_scales, second_gathered, 0)
        x_two = gather_words("x_two", x_table, two_list)
        d_k2 = gather_words("d_k2", d_table, k2_list)
        x_hy = gather_words("x_hy", x_table, hy_list)
        d_k3 = gather_words("d_k3", d_table, k3_list)
        d_k1 = gather_words("d_k1", d_table, k1_list)

        h_banks = [psum.tile([P, S], F32, name=f"h_bank{t}") for t in range(TILES)]
        early_bank = psum.tile([P, S], F32, name="early_bank", tag="first0")

        def second_pass(t, columns, codes, name, moving, moving_scales, start, stop):
            bank = early_bank if (t == 0 and columns == halves[0]) else h_banks[t]
            nc.tensor.matmul_mx(
                bank[:, columns], lhsT=codes[:, P * t : P * (t + 1)].bitcast(FP8X4),
                lhsT_scale=second_scales[:, place[name] + P * t : place[name] + P * (t + 1)],
                rhs=moving.bitcast(FP8X4), rhs_scale=moving_scales, start=start, stop=stop,
            )

        for codes, name, moving, moving_name in ((d_k2, "k2", x_two, "two"), (d_k3, "k3", x_hy, "hy")):
            for t in range(TILES):
                for columns in halves if t == 0 else [slice(0, S)]:
                    scales = second_scales[:, place[moving_name] + columns.start : place[moving_name] + columns.stop]
                    second_pass(t, columns, codes, name, moving[:, columns], scales, name == "k2", False)

        h2 = [sbuf(f"h2_{t}", [P, S], F32) for t in range(TILES)]
        bias = sbuf("bias", [P, PACK], F32)
        nc.vector.scalar_tensor_tensor(bias[:], slope[:], -1.0, threshold[:], ALU.mult, ALU.mult)
        weighted = sbuf("weighted", [P, TILES, S], F32)
        for t in range(TILES):
            nc.vector.tensor_scalar(weighted[:, t, :], ds2[t][:, 0:S], gain[:, t : t + 1], None, ALU.mult)

        for half, columns in enumerate(halves):
            sg = sbuf(f"sg{half}", [P, TILES, HALF], F32)
            z = sbuf(f"z{half}", [P, HALF * PACK], BF16)
            step = TILES // 2
            for first in range(0, TILES, step):
                group = slice(first, first + step)
                for t in range(first, first + step):
                    nc.scalar.activation(
                        sg[:, t, :], ds[t][:].indirect(n3_list[:, columns.start // 16 : columns.stop // 16]), ACT.Sigmoid,
                        bias=bias[:, t : t + 1], scale=slope[:, t : t + 1],
                    )
                nc.vector.tensor_tensor(
                    z[:].rearrange("p (c i t) -> p c t i", i=4, t=PACK)[:, :, group, :],
                    weighted[:, group, columns].rearrange("p t (c i) -> p c t i", i=4),
                    sg[:, group, :].rearrange("p t (c i) -> p c t i", i=4),
                    ALU.mult,
                )
            z_codes = sbuf(f"z_codes{half}", [P, HALF], U32)
            z_scales = sbuf(f"z_scales{half}", [P, HALF], U8)
            nc.vector.quantize_mx(z_codes[:].bitcast(FP8X4), z_scales[:], z[:])
            for t in range(TILES):
                second_pass(t, columns, d_k1, "k1", z_codes[:], z_scales[:], False, half == 1 or t == 0)
            if half == 0:
                nc.vector.tensor_scalar(h2[0][:, columns], early_bank[:, columns], 0.0625, None, ALU.mult)

        ub = [sbuf(f"ub{t}", [P, WIDE], F32) for t in range(TILES)]
        larger = [sbuf(f"larger{t}", [P, W], F32) for t in range(TILES)]
        smaller = [sbuf(f"smaller{t}", [P, W], F32) for t in range(TILES)]

        def fetch_pairs(t):
            columns = halves[1] if t == 0 else slice(0, S)
            nc.vector.tensor_scalar(h2[t][:, columns], h_banks[t][:, columns], 0.0625, None, ALU.mult)
            pa = sbuf(f"pa{t}", [P, W], F32)
            pb = sbuf(f"pb{t}", [P, W], F32)
            nc.scalar.activation(pa[:], h2[t][:].indirect(n4_list[:]), ACT.Copy)
            nc.scalar.activation(pb[:], h2[t][:].indirect(n5_list[:]), ACT.Copy)
            nc.vector.tensor_tensor(larger[t][:], pa[:], pb[:], ALU.max)
            nc.vector.tensor_tensor(smaller[t][:], pa[:], pb[:], ALU.min)

        def put_larger(t):
            nc.scalar.activation(ub[t][:].indirect(n4_list[:]), larger[t][:], ACT.Copy)

        def put_smaller(t):
            nc.scalar.activation(ub[t][:].indirect(n5_list[:]), smaller[t][:], ACT.Copy)

        def finish(t):
            width = HALF if t == TILES - 1 else S
            for start in range(0, S, width):
                columns = slice(start, start + width)
                fetched = sbuf(f"fetched{t}_{start}", [P, width], F32)
                nc.scalar.activation(fetched[:], ub[t][:].indirect(n6_list[:, start // 16 : (start + width) // 16]), ACT.Copy)
                result = sbuf(f"result{t}_{start}", [P, width], F32)
                nc.vector.tensor_tensor(result[:], ub[t][:, columns], fetched[:], ALU.subtract)
                nc.sync.dma_start(out[P * t : P * (t + 1), columns], result[:])

        for t in range(TILES):
            fetch_pairs(t)
        for pair in range(0, TILES, 2):
            put_larger(pair)
            put_larger(pair + 1)
            put_smaller(pair)
            put_smaller(pair + 1)
            finish(pair)
            finish(pair + 1)
